import numpy as np
import ml_dtypes


def mxq(x, axis, fmt="e4m3"):
    dtype, down = {"e4m3": (ml_dtypes.float8_e4m3fn, 7), "e5m2": (ml_dtypes.float8_e5m2, 14)}[fmt]
    v = np.moveaxis(np.asarray(x, np.float32).astype(ml_dtypes.bfloat16).astype(np.float64), axis, -1)
    blocks = v.reshape(v.shape[:-1] + (-1, 32))
    amax = np.abs(blocks).max(-1, keepdims=True)
    byte = np.maximum(np.where(amax > 0, np.frexp(amax)[1] - 1 + 127, 0) - down, 1)
    scale = np.exp2(byte - 127.0)
    codes = (blocks / scale).astype(np.float32).astype(dtype).astype(np.float64)
    return np.moveaxis((codes * scale).reshape(v.shape), -1, axis)


WIDE = False


def mx_kscale(k):
    if not WIDE:
        return np.ones(k)
    levels = np.array([10, -10, 5, -5, 0])
    if k % 512:
        return np.exp2(np.random.permutation(np.resize(levels, k // 32))).repeat(32)
    a = np.empty((k // 512, 16))
    for p in range(k // 512):
        a[p, :8] = np.random.permutation(np.resize(levels, 8))
        for g in range(8):
            far = levels[np.abs(levels - a[p, g]) >= 10]
            a[p, g + 8] = far[np.random.randint(len(far))]
    return np.exp2(a.ravel()).repeat(32)


BF16 = ml_dtypes.bfloat16


def bf(x):
    return np.asarray(x, np.float32).astype(BF16)


def f64(x):
    return np.asarray(x).astype(np.float64)


N, D, F = 6144, 1024, 512
H = F // 2


def max_min(h):
    hl = h[:, :H]
    hr = h[:, H:]
    return np.concatenate([np.maximum(hl, hr), np.minimum(hl, hr)], axis=1)


def draw0():
    a, u = mx_kscale(D), mx_kscale(F)
    return {
        "x": bf(np.random.standard_normal((N, D)) * a[None, :]),
        "w": bf(np.random.standard_normal((D, F)) / np.sqrt(D) / a[:, None]),
        "d": bf((1.0 + 0.2 * np.random.standard_normal(D)) * a * a),
        "s": bf((1.0 + 0.1 * np.random.standard_normal(F)) * u),
        "t": bf((1.0 + 0.1 * np.random.standard_normal(F)) / u),
        "b": bf(0.4 * np.random.standard_normal(F)),
    }


def core(x, w, d, s, t, b):
    x, w, d, s, t, b = f64(x), f64(w), f64(d), f64(s), f64(t), f64(b)
    wq = mxq(w, 0, "e4m3")
    p = mxq(x, 1, "e4m3") @ wq
    wd = d[:, None] * w
    g = mxq(wd, 0, "e4m3").T @ wq
    ps = p * s[None, :]
    gt = g * t[:, None]
    r = mxq(ps, 1, "e4m3") @ mxq(gt, 0, "e4m3")
    h = 1.5 * p - 0.5 * r + b[None, :]
    return max_min(h)


def e4m3fn_bytes(y):
    return np.clip(np.asarray(y, np.float64), -448.0, 448.0).astype(np.float32).astype(ml_dtypes.float8_e4m3fn).view(np.uint8)


def e4m3fn_values(b):
    return np.asarray(b, np.uint8).view(ml_dtypes.float8_e4m3fn).astype(np.float64)


def setup_inputs():
    d = draw0()
    x0 = np.asarray(d['x']).astype(np.float64)
    s = (np.max(np.abs(x0), axis=(0,), keepdims=True) / 448.0).astype(np.float32)
    out = {}
    for k, v in d.items():
        if k == 'x':
            out['x_bytes'] = e4m3fn_bytes(x0 / s.astype(np.float64))
            out['x_scale'] = s
        else:
            out[k] = v
    return out


def reference(x_bytes, x_scale, w, d, s, t, b):
    return core(e4m3fn_values(x_bytes) * x_scale.astype(np.float64), w, d, s, t, b)

@@ -1,0 +1,314 @@
+from contextlib import ExitStack
+
+import concourse.mybir as mybir
+from concourse.masks import make_identity
+
+N, D, F = 6144, 1024, 512
+FLOPS = 2 * N * D * F + 2 * D * F * F + 2 * N * F * F
+
+F32 = mybir.dt.float32
+BF16 = mybir.dt.bfloat16
+U32 = mybir.dt.uint32
+U8 = mybir.dt.uint8
+FP8 = mybir.dt.float8_e4m3fn
+FP8X4 = mybir.dt.float8_e4m3fn_x4
+MULT = mybir.AluOpType.mult
+ADD = mybir.AluOpType.add
+MAX = mybir.AluOpType.max
+MIN = mybir.AluOpType.min
+COPY = mybir.ActivationFunctionType.Copy
+IDENT = mybir.ActivationFunctionType.Identity
+
+P = 128
+UT = 256
+UNITS = N // UT
+GROUPS = N // 512
+V_ILV = 128
+
+
+def tile_bjorckmaxmindense_t_kernel(tc, x_bytes, x_scale, w, d, s, t, b, out):
+    nc = tc.nc
+    xv = x_bytes.rearrange("(n p j) k -> n p j k", p=P, j=4)
+    ov = out.rearrange("(n p j) c -> n p j c", p=P, j=4)
+    wv = w.rearrange("(g p j) c -> g p j c", p=P, j=4)
+
+    with ExitStack() as ctx:
+        const = ctx.enter_context(tc.tile_pool(name="const", bufs=1))
+        xin = ctx.enter_context(tc.tile_pool(name="xin", bufs=1))
+        work = ctx.enter_context(tc.tile_pool(name="work", bufs=3))
+        psum = ctx.enter_context(tc.psum_pool(name="psum", bufs=1))
+        ctx.enter_context(tc.manual_schedule())
+
+        sc = const.tile([P, 2, 4], F32, name="sc")
+        nc.scalar.dma_start(out=sc[:], in_=x_scale.rearrange("o (g p t) -> p (o g) t", g=2, t=4))
+        sb = const.tile([P, 4], BF16, name="sb")
+        tb = const.tile([P, 4], BF16, name="tb")
+        bb = const.tile([P, 4], BF16, name="bb")
+        db = const.tile([P, 2, 4], BF16, name="db")
+
+        xbytes = []
+        for n in range(GROUPS):
+            xbyte = xin.tile([P, 4, D], U8, name="xbyte%d" % n)
+            xbytes.append(xbyte)
+        w_raw = [const.tile([P, 4, F], BF16, name="w_raw%d" % g) for g in range(2)]
+        nc.sync.dma_start(out=xbytes[0][:, 0:2, :], in_=xv[0][:, 0:2, :])
+        for g in range(2):
+            nc.sync.dma_start(out=w_raw[g][:], in_=wv[g])
+        nc.sync.dma_start(out=xbytes[0][:, 2:4, :], in_=xv[0][:, 2:4, :])
+        nc.scalar.dma_start(out=db[:], in_=d.rearrange("(g p j) -> p g j", g=2, j=4))
+        nc.scalar.dma_start(out=sb[:], in_=s.rearrange("(p t) -> p t", t=4))
+        nc.scalar.dma_start(out=tb[:], in_=t.rearrange("(p t) -> p t", t=4))
+        nc.scalar.dma_start(out=bb[:], in_=b.rearrange("(p t) -> p t", t=4))
+        for n in range(1, GROUPS):
+            nc.sync.dma_start(out=xbytes[n][:], in_=xv[n])
+
+        dummy = const.tile([P, 1], F32, name="dummy")
+        dummy2 = const.tile([P, 1], F32, name="dummy2")
+        nc.vector.memset(dummy[:], 0.0)
+        nc.scalar.activation(out=dummy2[:], in_=dummy[:], func=IDENT, scale=1.0, bias=dummy[:])
+        ident = const.tile([P, P], F32, name="ident")
+        make_identity(nc, ident[:])
+
+        scol = const.tile([P, 4], F32, name="scol")
+        tcol = const.tile([P, 4], F32, name="tcol")
+        bcol = const.tile([P, 4], F32, name="bcol")
+        dcol = const.tile([P, 2, 4], F32, name="dcol")
+        w_codes = const.tile([P, 2, F], U32, name="w_codes", align_bytes=64)
+        w_scales = const.tile([P, 2, F], U8, name="w_scales", align_bytes=64)
+        wd_codes = const.tile([P, 2, F], U32, name="wd_codes", align_bytes=64)
+        wd_scales = const.tile([P, 2, F], U8, name="wd_scales", align_bytes=64)
+        gt_codes = const.tile([P, F], U32, name="gt_codes", align_bytes=64)
+        gt_scales = const.tile([P, F], U8, name="gt_scales", align_bytes=64)
+        wd_raw = [const.tile([P, 4, F], BF16, name="wd_raw%d" % g) for g in range(2)]
+        w_grp = [const.tile([P, 4, P, 4], BF16, name="w_grp%d" % g, align_bytes=64) for g in range(2)]
+        wd_grp = [const.tile([P, 4, P, 4], BF16, name="wd_grp%d" % g, align_bytes=64) for g in range(2)]
+        gt_planes = const.tile([P, 4, F], BF16, name="gt_planes")
+        gt_grp = const.tile([P, F, 4], BF16, name="gt_grp", align_bytes=64)
+
+        xbf, xt, xg, xc, xs = {}, {}, {}, {}, {}
+        pp, psp, psg, psc, pss, q, rr, z, oo, hr = {}, {}, {}, {}, {}, {}, {}, {}, {}, {}
+
+        def cast(u, on_scalar=()):
+            tile = work.tile([P, 2, D], BF16, name="xbf", bufs=4)
+            xbf[u] = tile
+            src = xbytes[u // 2]
+            h = 2 * (u % 2)
+            for j in range(2):
+                view = src[:, h + j, :].bitcast(FP8)
+                if j in on_scalar:
+                    nc.scalar.copy(out=tile[:, j, :], in_=view)
+                else:
+                    nc.gpsimd.tensor_copy(out=tile[:, j, :], in_=view)
+
+        def xtr(u):
+            xt[u] = []
+            for g in range(2):
+                bank = psum.tile([P, 2, UT], F32, name="xt%d" % g)
+                xt[u].append(bank)
+                for j in range(2):
+                    words = xbf[u][:, j, :].bitcast(F32)
+                    for h in range(2):
+                        nc.tensor.transpose(bank[:, h, j * P:(j + 1) * P], words[:, 256 * g + h:256 * (g + 1):2], ident[:])
+
+        def xmul(u, g):
+            if g == 0:
+                tile = work.tile([P, 2, UT, 2, 2], BF16, name="xg", align_bytes=64)
+                xg[u] = tile
+            nc.vector.tensor_tensor(
+                out=xg[u][:, g],
+                in0=xt[u][g][:].bitcast(BF16).rearrange("p u (r e) -> p r u e", e=2),
+                in1=sc[:, g, :].rearrange("p (u e) -> p u e", u=2).unsqueeze(1).to_broadcast([P, UT, 2, 2]),
+                op=MULT,
+            )
+
+        def xq(u):
+            xct = work.tile([P, 2, UT], U32, name="xct", align_bytes=64)
+            xst = work.tile([P, 2, UT], U8, name="xst", align_bytes=64)
+            xc[u], xs[u] = xct, xst
+            nc.vector.quantize_mx(
+                out=xct[:].rearrange("p g c -> p (g c)").bitcast(FP8X4),
+                scales=xst[:].rearrange("p g c -> p (g c)"),
+                in_=xg[u][:].rearrange("p g r u e -> p (g r u e)"),
+            )
+
+        def pmm(u):
+            pp[u] = []
+            for k in range(2):
+                bank = psum.tile([P, 2, UT], F32, name="pp%d" % k)
+                pp[u].append(bank)
+                for i in range(2):
+                    cols = slice(P * (2 * k + i), P * (2 * k + i + 1))
+                    for g in range(2):
+                        nc.tensor.matmul_mx(
+                            out=bank[:, i, :],
+                            lhsT=w_codes[:, g, cols].bitcast(FP8X4),
+                            lhsT_scale=w_scales[:, g, cols],
+                            rhs=xc[u][:, g, :].bitcast(FP8X4),
+                            rhs_scale=xs[u][:, g, :],
+                            start=(g == 0),
+                            stop=(g == 1),
+                        )
+
+        def ps(u):
+            tile = work.tile([P, 4, UT], BF16, name="psp")
+            psp[u] = tile
+            for k in range(4):
+                nc.scalar.activation(out=tile[:, k, :], in_=pp[u][k // 2][:, k % 2, :], func=COPY, scale=scol[:, k:k + 1])
+
+        def qq(u):
+            tile = work.tile([P, 4, UT], F32, name="q", bufs=4)
+            q[u] = tile
+            for k in range(4):
+                nc.scalar.activation(out=tile[:, k, :], in_=pp[u][k // 2][:, k % 2, :], func=IDENT, scale=1.5, bias=bcol[:, k:k + 1])
+
+        def ilv_scalar(u):
+            tile = work.tile([P, UT, 4], BF16, name="psg", align_bytes=64)
+            psg[u] = tile
+            if V_ILV < UT:
+                nc.scalar.copy(out=tile[:, V_ILV:, :], in_=psp[u][:, :, V_ILV:].rearrange("p k c -> p c k"))
+
+        def ilv_vector(u):
+            if V_ILV > 0:
+                nc.vector.tensor_copy(out=psg[u][:, :V_ILV, :], in_=psp[u][:, :, :V_ILV].rearrange("p k c -> p c k"))
+
+        def psquant(u):
+            pct = work.tile([P, UT], U32, name="pct", align_bytes=64)
+            pst = work.tile([P, UT], U8, name="pst", align_bytes=64)
+            psc[u], pss[u] = pct, pst
+            nc.vector.quantize_mx(out=pct[:].bitcast(FP8X4), scales=pst[:], in_=psg[u][:].rearrange("p c k -> p (c k)"))
+
+        def rmm(u):
+            rr[u] = []
+            for k in range(2):
+                bank = psum.tile([P, 2, UT], F32, name="rr%d" % k)
+                rr[u].append(bank)
+                for i in range(2):
+                    cols = slice(P * (2 * k + i), P * (2 * k + i + 1))
+                    nc.tensor.matmul_mx(
+                        out=bank[:, i, :],
+                        lhsT=gt_codes[:, cols].bitcast(FP8X4),
+                        lhsT_scale=gt_scales[:, cols],
+                        rhs=psc[u][:].bitcast(FP8X4),
+                        rhs_scale=pss[u][:],
+                        start=True,
+                        stop=True,
+                    )
+
+        def zz(u):
+            tile = work.tile([P, 4, UT], F32, name="z")
+            z[u] = tile
+            for k in range(2):
+                nc.scalar.activation(out=tile[:, 2 * k:2 * k + 2, :], in_=rr[u][k][:], func=COPY, scale=-0.5)
+
+        def otr(u):
+            oo[u] = []
+            for j in range(2):
+                bank = psum.tile([P, 4, P], F32, name="oo%d" % j)
+                oo[u].append(bank)
+                rows = slice(P * j, P * (j + 1))
+                for k in range(4):
+                    nc.tensor.matmul(out=bank[:, k, :], lhsT=q[u][:, k, rows], rhs=ident[:], is_transpose=True, start=True, stop=False)
+                    nc.tensor.matmul(out=bank[:, k, :], lhsT=z[u][:, k, rows], rhs=ident[:], is_transpose=True, start=False, stop=True)
+
+        def hrcopy(u):
+            tile = work.tile([P, 2, 64, 4], F32, name="hr")
+            hr[u] = tile
+            for j in range(2):
+                nc.scalar.copy(out=tile[:, j], in_=oo[u][j][:, :, 64:].rearrange("p k m -> p m k"))
+
+        def maxmin(u):
+            tile = work.tile([P, 2, F], F32, name="ot")
+            for j in range(2):
+                left = oo[u][j][:, :, :64].rearrange("p k m -> p m k")
+                for half, op in ((0, MAX), (1, MIN)):
+                    nc.vector.tensor_tensor(
+                        out=tile[:, j, 256 * half:256 * (half + 1)].rearrange("p (m k) -> p m k", k=4),
+                        in0=left,
+                        in1=hr[u][:, j],
+                        op=op,
+                    )
+            h = 2 * (u % 2)
+            nc.sync.dma_start(out=ov[u // 2][:, h:h + 2, :], in_=tile[:])
+
+        def wquant(codes, scales, grp, g):
+            nc.vector.quantize_mx(out=codes[:, g, :].bitcast(FP8X4), scales=scales[:, g, :], in_=grp[g][:].rearrange("p t m j -> p (t m j)"))
+
+        def wilv(engine_copy, grp, raw, g):
+            engine_copy(out=grp[g][:], in_=raw[g][:].rearrange("p j (m t) -> p t m j", t=4))
+
+        cast(0, on_scalar=(1,))
+        cast(1)
+        cast(2)
+        xtr(0)
+        nc.vector.tensor_copy(out=dcol[:], in_=db[:])
+        nc.vector.tensor_copy(out=scol[:], in_=sb[:])
+        nc.vector.tensor_copy(out=tcol[:], in_=tb[:])
+        nc.vector.tensor_copy(out=bcol[:], in_=bb[:])
+        xmul(0, 0)
+        wilv(nc.vector.tensor_copy, w_grp, w_raw, 0)
+        wilv(nc.scalar.copy, w_grp, w_raw, 1)
+        xmul(0, 1)
+        wquant(w_codes, w_scales, w_grp, 0)
+        wquant(w_codes, w_scales, w_grp, 1)
+        xq(0)
+        for g in range(2):
+            for j in range(4):
+                nc.vector.tensor_scalar(out=wd_raw[g][:, j, :], in0=w_raw[g][:, j, :], scalar1=dcol[:, g, j:j + 1], scalar2=None, op0=MULT)
+        wilv(nc.scalar.copy, wd_grp, wd_raw, 1)
+        wilv(nc.vector.tensor_copy, wd_grp, wd_raw, 0)
+
+        for slot in range(UNITS + 2):
+            u_next, u_r, u_o = slot + 1, slot - 1, slot - 2
+            if slot + 3 < UNITS:
+                cast(slot + 3)
+            if u_next < UNITS:
+                xtr(u_next)
+            if 0 <= u_o < UNITS:
+                otr(u_o)
+                hrcopy(u_o)
+            if 0 <= u_r < UNITS:
+                ilv_vector(u_r)
+            if u_next < UNITS:
+                xmul(u_next, 0)
+            if slot == 0:
+                wquant(wd_codes, wd_scales, wd_grp, 0)
+                wquant(wd_codes, wd_scales, wd_grp, 1)
+            if slot == 1:
+                nc.vector.tensor_copy(out=gt_grp[:], in_=gt_planes[:].rearrange("p k c -> p c k"))
+            if 0 <= u_r < UNITS:
+                psquant(u_r)
+            if slot == 1:
+                nc.vector.quantize_mx(out=gt_codes[:].bitcast(FP8X4), scales=gt_scales[:], in_=gt_grp[:].rearrange("p c k -> p (c k)"))
+            if u_next < UNITS:
+                xmul(u_next, 1)
+            if 0 <= u_r < UNITS:
+                rmm(u_r)
+            if slot < UNITS:
+                pmm(slot)
+            if 0 <= u_r < UNITS:
+                zz(u_r)
+            if slot < UNITS:
+                ps(slot)
+                ilv_scalar(slot)
+                qq(slot)
+            if slot == 0:
+                gbank = []
+                for k in range(4):
+                    bank = psum.tile([P, F], F32, name="gb%d" % k, tag=("rr0", "rr1", "oo0", "oo1")[k])
+                    gbank.append(bank)
+                    for g in range(2):
+                        nc.tensor.matmul_mx(
+                            out=bank[:],
+                            lhsT=wd_codes[:, g, P * k:P * (k + 1)].bitcast(FP8X4),
+                            lhsT_scale=wd_scales[:, g, P * k:P * (k + 1)],
+                            rhs=w_codes[:, g, :].bitcast(FP8X4),
+                            rhs_scale=w_scales[:, g, :],
+                            start=(g == 0),
+                            stop=(g == 1),
+                        )
+                for k in range(4):
+                    nc.scalar.activation(out=gt_planes[:, k, :], in_=gbank[k][:], func=COPY, scale=tcol[:, k:k + 1])
+            if 0 <= u_o < UNITS:
+                maxmin(u_o)
+            if u_next < UNITS:
+                xq(u_next)

@@ -20,10 +20,26 @@ COPY = mybir.ActivationFunctionType.Copy
 IDENT = mybir.ActivationFunctionType.Identity
 
 P = 128
+CUT = 640
 UT = 256
 UNITS = N // UT
 GROUPS = N // 512
-V_ILV = 128
+
+
+def cast_engine(u, j):
+    return (("S", 0, D),) if j == 0 else (("S", 0, CUT), ("V", CUT, D))
+
+
+def ps_engine(u, k):
+    return "V" if u >= UNITS - 1 else "G"
+
+
+def z_engine(u, k):
+    return "V" if u == UNITS - 1 and k >= 2 else "S"
+
+
+def ilv_engine(u):
+    return "V" if u >= UNITS - 1 else "G"
 
 
 def tile_bjorckmaxmindense_t_kernel(tc, x_bytes, x_scale, w, d, s, t, b, out):
@@ -86,19 +102,22 @@ def tile_bjorckmaxmindense_t_kernel(tc, x_bytes, x_scale, w, d, s, t, b, out):
         gt_grp = const.tile([P, F, 4], BF16, name="gt_grp", align_bytes=64)
 
         xbf, xt, xg, xc, xs = {}, {}, {}, {}, {}
-        pp, psp, psg, psc, pss, q, rr, z, oo, hr = {}, {}, {}, {}, {}, {}, {}, {}, {}, {}
+        pp, pf, psp, psg, psc, pss, rr, z, oo, hr = {}, {}, {}, {}, {}, {}, {}, {}, {}, {}
 
-        def cast(u, on_scalar=()):
-            tile = work.tile([P, 2, D], BF16, name="xbf", bufs=4)
-            xbf[u] = tile
+        def cast(u, j):
+            if j == 0:
+                tile = work.tile([P, 2, D], BF16, name="xbf", bufs=5)
+                xbf[u] = tile
             src = xbytes[u // 2]
-            h = 2 * (u % 2)
-            for j in range(2):
-                view = src[:, h + j, :].bitcast(FP8)
-                if j in on_scalar:
-                    nc.scalar.copy(out=tile[:, j, :], in_=view)
+            for eng, c0, c1 in cast_engine(u, j):
+                dst = xbf[u][:, j, c0:c1]
+                view = src[:, 2 * (u % 2) + j, c0:c1].bitcast(FP8)
+                if eng == "S":
+                    nc.scalar.copy(out=dst, in_=view)
+                elif eng == "V":
+                    nc.vector.tensor_copy(out=dst, in_=view)
                 else:
-                    nc.gpsimd.tensor_copy(out=tile[:, j, :], in_=view)
+                    nc.gpsimd.tensor_copy(out=dst, in_=view)
 
         def xtr(u):
             xt[u] = []
@@ -149,27 +168,34 @@ def tile_bjorckmaxmindense_t_kernel(tc, x_bytes, x_scale, w, d, s, t, b, out):
                             stop=(g == 1),
                         )
 
+        def pout(u):
+            tile = work.tile([P, 4, UT], F32, name="pf", bufs=6)
+            pf[u] = tile
+            for k in range(2):
+                nc.scalar.copy(out=tile[:, 2 * k:2 * k + 2, :], in_=pp[u][k][:])
+
         def ps(u):
             tile = work.tile([P, 4, UT], BF16, name="psp")
             psp[u] = tile
             for k in range(4):
-                nc.scalar.activation(out=tile[:, k, :], in_=pp[u][k // 2][:, k % 2, :], func=COPY, scale=scol[:, k:k + 1])
+                if ps_engine(u, k) == "V":
+                    nc.vector.tensor_scalar(out=tile[:, k, :], in0=pf[u][:, k, :], scalar1=scol[:, k:k + 1], scalar2=None, op0=MULT)
+                elif ps_engine(u, k) == "S":
+                    nc.scalar.activation(out=tile[:, k, :], in_=pf[u][:, k, :], func=COPY, scale=scol[:, k:k + 1])
+                else:
+                    nc.gpsimd.tensor_scalar(out=tile[:, k, :], in0=pf[u][:, k, :], scalar1=scol[:, k:k + 1], scalar2=0.0, op0=MULT, op1=ADD)
 
-        def qq(u):
-            tile = work.tile([P, 4, UT], F32, name="q", bufs=4)
-            q[u] = tile
-            for k in range(4):
-                nc.scalar.activation(out=tile[:, k, :], in_=pp[u][k // 2][:, k % 2, :], func=IDENT, scale=1.5, bias=bcol[:, k:k + 1])
-
-        def ilv_scalar(u):
+        def ilv(u):
             tile = work.tile([P, UT, 4], BF16, name="psg", align_bytes=64)
             psg[u] = tile
-            if V_ILV < UT:
-                nc.scalar.copy(out=tile[:, V_ILV:, :], in_=psp[u][:, :, V_ILV:].rearrange("p k c -> p c k"))
-
-        def ilv_vector(u):
-            if V_ILV > 0:
-                nc.vector.tensor_copy(out=psg[u][:, :V_ILV, :], in_=psp[u][:, :, :V_ILV].rearrange("p k c -> p c k"))
+            src = psp[u][:].rearrange("p k c -> p c k")
+            if ilv_engine(u) == "V":
+                nc.vector.tensor_copy(out=tile[:], in_=src)
+            elif ilv_engine(u) == "S":
+                nc.scalar.copy(out=tile[:], in_=src)
+            else:
+                for c in range(0, UT, 128):
+                    nc.gpsimd.tensor_scalar(out=tile[:, c:c + 128, :], in0=src[:, c:c + 128, :], scalar1=1.0, scalar2=0.0, op0=MULT, op1=ADD)
 
         def psquant(u):
             pct = work.tile([P, UT], U32, name="pct", align_bytes=64)
@@ -197,8 +223,12 @@ def tile_bjorckmaxmindense_t_kernel(tc, x_bytes, x_scale, w, d, s, t, b, out):
         def zz(u):
             tile = work.tile([P, 4, UT], F32, name="z")
             z[u] = tile
-            for k in range(2):
-                nc.scalar.activation(out=tile[:, 2 * k:2 * k + 2, :], in_=rr[u][k][:], func=COPY, scale=-0.5)
+            for k in range(4):
+                src = rr[u][k // 2][:, k % 2, :]
+                if z_engine(u, k) == "S":
+                    nc.scalar.activation(out=tile[:, k, :], in_=src, func=IDENT, scale=-1.0 / 3.0, bias=bcol[:, k:k + 1])
+                else:
+                    nc.vector.tensor_scalar(out=tile[:, k, :], in0=src, scalar1=-1.0 / 3.0, scalar2=bcol[:, k:k + 1], op0=MULT, op1=ADD)
 
         def otr(u):
             oo[u] = []
@@ -207,25 +237,27 @@ def tile_bjorckmaxmindense_t_kernel(tc, x_bytes, x_scale, w, d, s, t, b, out):
                 oo[u].append(bank)
                 rows = slice(P * j, P * (j + 1))
                 for k in range(4):
-                    nc.tensor.matmul(out=bank[:, k, :], lhsT=q[u][:, k, rows], rhs=ident[:], is_transpose=True, start=True, stop=False)
+                    nc.tensor.matmul(out=bank[:, k, :], lhsT=pf[u][:, k, rows], rhs=ident[:], is_transpose=True, start=True, stop=False)
                     nc.tensor.matmul(out=bank[:, k, :], lhsT=z[u][:, k, rows], rhs=ident[:], is_transpose=True, start=False, stop=True)
 
         def hrcopy(u):
             tile = work.tile([P, 2, 64, 4], F32, name="hr")
             hr[u] = tile
             for j in range(2):
-                nc.scalar.copy(out=tile[:, j], in_=oo[u][j][:, :, 64:].rearrange("p k m -> p m k"))
+                nc.scalar.activation(out=tile[:, j], in_=oo[u][j][:, :, 64:].rearrange("p k m -> p m k"), func=COPY, scale=1.5)
 
         def maxmin(u):
             tile = work.tile([P, 2, F], F32, name="ot")
             for j in range(2):
                 left = oo[u][j][:, :, :64].rearrange("p k m -> p m k")
                 for half, op in ((0, MAX), (1, MIN)):
-                    nc.vector.tensor_tensor(
+                    nc.vector.scalar_tensor_tensor(
                         out=tile[:, j, 256 * half:256 * (half + 1)].rearrange("p (m k) -> p m k", k=4),
                         in0=left,
+                        scalar=1.5,
                         in1=hr[u][:, j],
-                        op=op,
+                        op0=MULT,
+                        op1=op,
                     )
             h = 2 * (u % 2)
             nc.sync.dma_start(out=ov[u // 2][:, h:h + 2, :], in_=tile[:])
@@ -233,65 +265,45 @@ def tile_bjorckmaxmindense_t_kernel(tc, x_bytes, x_scale, w, d, s, t, b, out):
         def wquant(codes, scales, grp, g):
             nc.vector.quantize_mx(out=codes[:, g, :].bitcast(FP8X4), scales=scales[:, g, :], in_=grp[g][:].rearrange("p t m j -> p (t m j)"))
 
-        def wilv(engine_copy, grp, raw, g):
-            engine_copy(out=grp[g][:], in_=raw[g][:].rearrange("p j (m t) -> p t m j", t=4))
-
-        cast(0, on_scalar=(1,))
-        cast(1)
-        cast(2)
-        xtr(0)
-        nc.vector.tensor_copy(out=dcol[:], in_=db[:])
-        nc.vector.tensor_copy(out=scol[:], in_=sb[:])
-        nc.vector.tensor_copy(out=tcol[:], in_=tb[:])
-        nc.vector.tensor_copy(out=bcol[:], in_=bb[:])
-        xmul(0, 0)
-        wilv(nc.vector.tensor_copy, w_grp, w_raw, 0)
-        wilv(nc.scalar.copy, w_grp, w_raw, 1)
-        xmul(0, 1)
-        wquant(w_codes, w_scales, w_grp, 0)
-        wquant(w_codes, w_scales, w_grp, 1)
-        xq(0)
-        for g in range(2):
+        def wd_mul(g):
             for j in range(4):
                 nc.vector.tensor_scalar(out=wd_raw[g][:, j, :], in0=w_raw[g][:, j, :], scalar1=dcol[:, g, j:j + 1], scalar2=None, op0=MULT)
-        wilv(nc.scalar.copy, wd_grp, wd_raw, 1)
-        wilv(nc.vector.tensor_copy, wd_grp, wd_raw, 0)
 
-        for slot in range(UNITS + 2):
-            u_next, u_r, u_o = slot + 1, slot - 1, slot - 2
+        def w_view(tile):
+            return tile[:].rearrange("p j (m t) -> p t m j", t=4)
+
+        cast(0, 0)
+        cast(0, 1)
+        nc.vector.tensor_copy(out=w_grp[0][:], in_=w_view(w_raw[0]))
+        for k in range(4):
+            nc.gpsimd.tensor_scalar(out=w_grp[1][:, k], in0=w_view(w_raw[1])[:, k], scalar1=1.0, scalar2=0.0, op0=MULT, op1=ADD)
+        xtr(0)
+        xmul(0, 0)
+        nc.vector.tensor_copy(out=dcol[:], in_=db[:])
+        xmul(0, 1)
+        wquant(w_codes, w_scales, w_grp, 0)
+        wd_mul(0)
+        xq(0)
+        wquant(w_codes, w_scales, w_grp, 1)
+        wd_mul(1)
+        for k in range(4):
+            nc.gpsimd.tensor_scalar(out=wd_grp[0][:, k], in0=w_view(wd_raw[0])[:, k], scalar1=1.0, scalar2=0.0, op0=MULT, op1=ADD)
+        cast(1, 0)
+        cast(1, 1)
+        cast(2, 0)
+        cast(2, 1)
+        nc.scalar.copy(out=wd_grp[1][:], in_=w_view(wd_raw[1]))
+        nc.vector.tensor_copy(out=scol[:], in_=sb[:])
+        nc.vector.tensor_copy(out=tcol[:], in_=tb[:])
+        nc.vector.tensor_scalar(out=bcol[:], in0=bb[:], scalar1=1.0 / 1.5, scalar2=None, op0=MULT)
+
+        for slot in range(UNITS + 3):
+            u_next, u_p, u_s, u_r, u_o = slot + 1, slot, slot - 1, slot - 2, slot - 3
             if slot + 3 < UNITS:
-                cast(slot + 3)
+                cast(slot + 3, 0)
             if u_next < UNITS:
                 xtr(u_next)
-            if 0 <= u_o < UNITS:
-                otr(u_o)
-                hrcopy(u_o)
-            if 0 <= u_r < UNITS:
-                ilv_vector(u_r)
-            if u_next < UNITS:
-                xmul(u_next, 0)
-            if slot == 0:
-                wquant(wd_codes, wd_scales, wd_grp, 0)
-                wquant(wd_codes, wd_scales, wd_grp, 1)
             if slot == 1:
-                nc.vector.tensor_copy(out=gt_grp[:], in_=gt_planes[:].rearrange("p k c -> p c k"))
-            if 0 <= u_r < UNITS:
-                psquant(u_r)
-            if slot == 1:
-                nc.vector.quantize_mx(out=gt_codes[:].bitcast(FP8X4), scales=gt_scales[:], in_=gt_grp[:].rearrange("p c k -> p (c k)"))
-            if u_next < UNITS:
-                xmul(u_next, 1)
-            if 0 <= u_r < UNITS:
-                rmm(u_r)
-            if slot < UNITS:
-                pmm(slot)
-            if 0 <= u_r < UNITS:
-                zz(u_r)
-            if slot < UNITS:
-                ps(slot)
-                ilv_scalar(slot)
-                qq(slot)
-            if slot == 0:
                 gbank = []
                 for k in range(4):
                     bank = psum.tile([P, F], F32, name="gb%d" % k, tag=("rr0", "rr1", "oo0", "oo1")[k])
@@ -308,7 +320,32 @@ def tile_bjorckmaxmindense_t_kernel(tc, x_bytes, x_scale, w, d, s, t, b, out):
                         )
                 for k in range(4):
                     nc.scalar.activation(out=gt_planes[:, k, :], in_=gbank[k][:], func=COPY, scale=tcol[:, k:k + 1])
+            if 0 <= u_s < UNITS:
+                ps(u_s)
+                ilv(u_s)
+            if 0 <= u_o < UNITS:
+                otr(u_o)
+                hrcopy(u_o)
+            if slot == 2:
+                nc.vector.tensor_copy(out=gt_grp[:], in_=gt_planes[:].rearrange("p k c -> p c k"))
+                nc.vector.quantize_mx(out=gt_codes[:].bitcast(FP8X4), scales=gt_scales[:], in_=gt_grp[:].rearrange("p c k -> p (c k)"))
+            if u_next < UNITS:
+                xmul(u_next, 0)
+                xmul(u_next, 1)
+            if slot == 0:
+                wquant(wd_codes, wd_scales, wd_grp, 0)
+                wquant(wd_codes, wd_scales, wd_grp, 1)
+            if 0 <= u_r < UNITS:
+                rmm(u_r)
+                zz(u_r)
+            if u_p < UNITS:
+                pmm(u_p)
+                pout(u_p)
+            if slot + 3 < UNITS:
+                cast(slot + 3, 1)
             if 0 <= u_o < UNITS:
                 maxmin(u_o)
             if u_next < UNITS:
                 xq(u_next)
+            if 0 <= u_s < UNITS:
+                psquant(u_s)

from contextlib import ExitStack

import concourse.mybir as mybir
from concourse.masks import make_identity

N, D, F = 6144, 1024, 512
FLOPS = 2 * N * D * F + 2 * D * F * F + 2 * N * F * F

F32 = mybir.dt.float32
BF16 = mybir.dt.bfloat16
U32 = mybir.dt.uint32
U8 = mybir.dt.uint8
FP8 = mybir.dt.float8_e4m3fn
FP8X4 = mybir.dt.float8_e4m3fn_x4
MULT = mybir.AluOpType.mult
ADD = mybir.AluOpType.add
MAX = mybir.AluOpType.max
MIN = mybir.AluOpType.min
COPY = mybir.ActivationFunctionType.Copy
IDENT = mybir.ActivationFunctionType.Identity

P = 128
CUT = 640
UT = 256
UNITS = N // UT
GROUPS = N // 512


def cast_engine(u, j):
    return (("S", 0, D),) if j == 0 else (("S", 0, CUT), ("V", CUT, D))


def ps_engine(u, k):
    return "V" if u >= UNITS - 1 else "G"


def z_engine(u, k):
    return "V" if u == UNITS - 1 and k >= 2 else "S"


def ilv_engine(u):
    return "V" if u >= UNITS - 1 else "G"


def tile_bjorckmaxmindense_t_kernel(tc, x_bytes, x_scale, w, d, s, t, b, out):
    nc = tc.nc
    xv = x_bytes.rearrange("(n p j) k -> n p j k", p=P, j=4)
    ov = out.rearrange("(n p j) c -> n p j c", p=P, j=4)
    wv = w.rearrange("(g p j) c -> g p j c", p=P, j=4)

    with ExitStack() as ctx:
        const = ctx.enter_context(tc.tile_pool(name="const", bufs=1))
        xin = ctx.enter_context(tc.tile_pool(name="xin", bufs=1))
        work = ctx.enter_context(tc.tile_pool(name="work", bufs=3))
        psum = ctx.enter_context(tc.psum_pool(name="psum", bufs=1))
        ctx.enter_context(tc.manual_schedule())

        sc = const.tile([P, 2, 4], F32, name="sc")
        nc.scalar.dma_start(out=sc[:], in_=x_scale.rearrange("o (g p t) -> p (o g) t", g=2, t=4))
        sb = const.tile([P, 4], BF16, name="sb")
        tb = const.tile([P, 4], BF16, name="tb")
        bb = const.tile([P, 4], BF16, name="bb")
        db = const.tile([P, 2, 4], BF16, name="db")

        xbytes = []
        for n in range(GROUPS):
            xbyte = xin.tile([P, 4, D], U8, name="xbyte%d" % n)
            xbytes.append(xbyte)
        w_raw = [const.tile([P, 4, F], BF16, name="w_raw%d" % g) for g in range(2)]
        nc.sync.dma_start(out=xbytes[0][:, 0:2, :], in_=xv[0][:, 0:2, :])
        for g in range(2):
            nc.sync.dma_start(out=w_raw[g][:], in_=wv[g])
        nc.sync.dma_start(out=xbytes[0][:, 2:4, :], in_=xv[0][:, 2:4, :])
        nc.scalar.dma_start(out=db[:], in_=d.rearrange("(g p j) -> p g j", g=2, j=4))
        nc.scalar.dma_start(out=sb[:], in_=s.rearrange("(p t) -> p t", t=4))
        nc.scalar.dma_start(out=tb[:], in_=t.rearrange("(p t) -> p t", t=4))
        nc.scalar.dma_start(out=bb[:], in_=b.rearrange("(p t) -> p t", t=4))
        for n in range(1, GROUPS):
            nc.sync.dma_start(out=xbytes[n][:], in_=xv[n])

        dummy = const.tile([P, 1], F32, name="dummy")
        dummy2 = const.tile([P, 1], F32, name="dummy2")
        nc.vector.memset(dummy[:], 0.0)
        nc.scalar.activation(out=dummy2[:], in_=dummy[:], func=IDENT, scale=1.0, bias=dummy[:])
        ident = const.tile([P, P], F32, name="ident")
        make_identity(nc, ident[:])

        scol = const.tile([P, 4], F32, name="scol")
        tcol = const.tile([P, 4], F32, name="tcol")
        bcol = const.tile([P, 4], F32, name="bcol")
        dcol = const.tile([P, 2, 4], F32, name="dcol")
        w_codes = const.tile([P, 2, F], U32, name="w_codes", align_bytes=64)
        w_scales = const.tile([P, 2, F], U8, name="w_scales", align_bytes=64)
        wd_codes = const.tile([P, 2, F], U32, name="wd_codes", align_bytes=64)
        wd_scales = const.tile([P, 2, F], U8, name="wd_scales", align_bytes=64)
        gt_codes = const.tile([P, F], U32, name="gt_codes", align_bytes=64)
        gt_scales = const.tile([P, F], U8, name="gt_scales", align_bytes=64)
        wd_raw = [const.tile([P, 4, F], BF16, name="wd_raw%d" % g) for g in range(2)]
        w_grp = [const.tile([P, 4, P, 4], BF16, name="w_grp%d" % g, align_bytes=64) for g in range(2)]
        wd_grp = [const.tile([P, 4, P, 4], BF16, name="wd_grp%d" % g, align_bytes=64) for g in range(2)]
        gt_planes = const.tile([P, 4, F], BF16, name="gt_planes")
        gt_grp = const.tile([P, F, 4], BF16, name="gt_grp", align_bytes=64)

        xbf, xt, xg, xc, xs = {}, {}, {}, {}, {}
        pp, pf, psp, psg, psc, pss, rr, z, oo, hr = {}, {}, {}, {}, {}, {}, {}, {}, {}, {}

        def cast(u, j):
            if j == 0:
                tile = work.tile([P, 2, D], BF16, name="xbf", bufs=5)
                xbf[u] = tile
            src = xbytes[u // 2]
            for eng, c0, c1 in cast_engine(u, j):
                dst = xbf[u][:, j, c0:c1]
                view = src[:, 2 * (u % 2) + j, c0:c1].bitcast(FP8)
                if eng == "S":
                    nc.scalar.copy(out=dst, in_=view)
                elif eng == "V":
                    nc.vector.tensor_copy(out=dst, in_=view)
                else:
                    nc.gpsimd.tensor_copy(out=dst, in_=view)

        def xtr(u):
            xt[u] = []
            for g in range(2):
                bank = psum.tile([P, 2, UT], F32, name="xt%d" % g)
                xt[u].append(bank)
                for j in range(2):
                    words = xbf[u][:, j, :].bitcast(F32)
                    for h in range(2):
                        nc.tensor.transpose(bank[:, h, j * P:(j + 1) * P], words[:, 256 * g + h:256 * (g + 1):2], ident[:])

        def xmul(u, g):
            if g == 0:
                tile = work.tile([P, 2, UT, 2, 2], BF16, name="xg", align_bytes=64)
                xg[u] = tile
            nc.vector.tensor_tensor(
                out=xg[u][:, g],
                in0=xt[u][g][:].bitcast(BF16).rearrange("p u (r e) -> p r u e", e=2),
                in1=sc[:, g, :].rearrange("p (u e) -> p u e", u=2).unsqueeze(1).to_broadcast([P, UT, 2, 2]),
                op=MULT,
            )

        def xq(u):
            xct = work.tile([P, 2, UT], U32, name="xct", align_bytes=64)
            xst = work.tile([P, 2, UT], U8, name="xst", align_bytes=64)
            xc[u], xs[u] = xct, xst
            nc.vector.quantize_mx(
                out=xct[:].rearrange("p g c -> p (g c)").bitcast(FP8X4),
                scales=xst[:].rearrange("p g c -> p (g c)"),
                in_=xg[u][:].rearrange("p g r u e -> p (g r u e)"),
            )

        def pmm(u):
            pp[u] = []
            for k in range(2):
                bank = psum.tile([P, 2, UT], F32, name="pp%d" % k)
                pp[u].append(bank)
                for i in range(2):
                    cols = slice(P * (2 * k + i), P * (2 * k + i + 1))
                    for g in range(2):
                        nc.tensor.matmul_mx(
                            out=bank[:, i, :],
                            lhsT=w_codes[:, g, cols].bitcast(FP8X4),
                            lhsT_scale=w_scales[:, g, cols],
                            rhs=xc[u][:, g, :].bitcast(FP8X4),
                            rhs_scale=xs[u][:, g, :],
                            start=(g == 0),
                            stop=(g == 1),
                        )

        def pout(u):
            tile = work.tile([P, 4, UT], F32, name="pf", bufs=6)
            pf[u] = tile
            for k in range(2):
                nc.scalar.copy(out=tile[:, 2 * k:2 * k + 2, :], in_=pp[u][k][:])

        def ps(u):
            tile = work.tile([P, 4, UT], BF16, name="psp")
            psp[u] = tile
            for k in range(4):
                if ps_engine(u, k) == "V":
                    nc.vector.tensor_scalar(out=tile[:, k, :], in0=pf[u][:, k, :], scalar1=scol[:, k:k + 1], scalar2=None, op0=MULT)
                elif ps_engine(u, k) == "S":
                    nc.scalar.activation(out=tile[:, k, :], in_=pf[u][:, k, :], func=COPY, scale=scol[:, k:k + 1])
                else:
                    nc.gpsimd.tensor_scalar(out=tile[:, k, :], in0=pf[u][:, k, :], scalar1=scol[:, k:k + 1], scalar2=0.0, op0=MULT, op1=ADD)

        def ilv(u):
            tile = work.tile([P, UT, 4], BF16, name="psg", align_bytes=64)
            psg[u] = tile
            src = psp[u][:].rearrange("p k c -> p c k")
            if ilv_engine(u) == "V":
                nc.vector.tensor_copy(out=tile[:], in_=src)
            elif ilv_engine(u) == "S":
                nc.scalar.copy(out=tile[:], in_=src)
            else:
                for c in range(0, UT, 128):
                    nc.gpsimd.tensor_scalar(out=tile[:, c:c + 128, :], in0=src[:, c:c + 128, :], scalar1=1.0, scalar2=0.0, op0=MULT, op1=ADD)

        def psquant(u):
            pct = work.tile([P, UT], U32, name="pct", align_bytes=64)
            pst = work.tile([P, UT], U8, name="pst", align_bytes=64)
            psc[u], pss[u] = pct, pst
            nc.vector.quantize_mx(out=pct[:].bitcast(FP8X4), scales=pst[:], in_=psg[u][:].rearrange("p c k -> p (c k)"))

        def rmm(u):
            rr[u] = []
            for k in range(2):
                bank = psum.tile([P, 2, UT], F32, name="rr%d" % k)
                rr[u].append(bank)
                for i in range(2):
                    cols = slice(P * (2 * k + i), P * (2 * k + i + 1))
                    nc.tensor.matmul_mx(
                        out=bank[:, i, :],
                        lhsT=gt_codes[:, cols].bitcast(FP8X4),
                        lhsT_scale=gt_scales[:, cols],
                        rhs=psc[u][:].bitcast(FP8X4),
                        rhs_scale=pss[u][:],
                        start=True,
                        stop=True,
                    )

        def zz(u):
            tile = work.tile([P, 4, UT], F32, name="z")
            z[u] = tile
            for k in range(4):
                src = rr[u][k // 2][:, k % 2, :]
                if z_engine(u, k) == "S":
                    nc.scalar.activation(out=tile[:, k, :], in_=src, func=IDENT, scale=-1.0 / 3.0, bias=bcol[:, k:k + 1])
                else:
                    nc.vector.tensor_scalar(out=tile[:, k, :], in0=src, scalar1=-1.0 / 3.0, scalar2=bcol[:, k:k + 1], op0=MULT, op1=ADD)

        def otr(u):
            oo[u] = []
            for j in range(2):
                bank = psum.tile([P, 4, P], F32, name="oo%d" % j)
                oo[u].append(bank)
                rows = slice(P * j, P * (j + 1))
                for k in range(4):
                    nc.tensor.matmul(out=bank[:, k, :], lhsT=pf[u][:, k, rows], rhs=ident[:], is_transpose=True, start=True, stop=False)
                    nc.tensor.matmul(out=bank[:, k, :], lhsT=z[u][:, k, rows], rhs=ident[:], is_transpose=True, start=False, stop=True)

        def hrcopy(u):
            tile = work.tile([P, 2, 64, 4], F32, name="hr")
            hr[u] = tile
            for j in range(2):
                nc.scalar.activation(out=tile[:, j], in_=oo[u][j][:, :, 64:].rearrange("p k m -> p m k"), func=COPY, scale=1.5)

        def maxmin(u):
            tile = work.tile([P, 2, F], F32, name="ot")
            for j in range(2):
                left = oo[u][j][:, :, :64].rearrange("p k m -> p m k")
                for half, op in ((0, MAX), (1, MIN)):
                    nc.vector.scalar_tensor_tensor(
                        out=tile[:, j, 256 * half:256 * (half + 1)].rearrange("p (m k) -> p m k", k=4),
                        in0=left,
                        scalar=1.5,
                        in1=hr[u][:, j],
                        op0=MULT,
                        op1=op,
                    )
            h = 2 * (u % 2)
            nc.sync.dma_start(out=ov[u // 2][:, h:h + 2, :], in_=tile[:])

        def wquant(codes, scales, grp, g):
            nc.vector.quantize_mx(out=codes[:, g, :].bitcast(FP8X4), scales=scales[:, g, :], in_=grp[g][:].rearrange("p t m j -> p (t m j)"))

        def wd_mul(g):
            for j in range(4):
                nc.vector.tensor_scalar(out=wd_raw[g][:, j, :], in0=w_raw[g][:, j, :], scalar1=dcol[:, g, j:j + 1], scalar2=None, op0=MULT)

        def w_view(tile):
            return tile[:].rearrange("p j (m t) -> p t m j", t=4)

        cast(0, 0)
        cast(0, 1)
        nc.vector.tensor_copy(out=w_grp[0][:], in_=w_view(w_raw[0]))
        for k in range(4):
            nc.gpsimd.tensor_scalar(out=w_grp[1][:, k], in0=w_view(w_raw[1])[:, k], scalar1=1.0, scalar2=0.0, op0=MULT, op1=ADD)
        xtr(0)
        xmul(0, 0)
        nc.vector.tensor_copy(out=dcol[:], in_=db[:])
        xmul(0, 1)
        wquant(w_codes, w_scales, w_grp, 0)
        wd_mul(0)
        xq(0)
        wquant(w_codes, w_scales, w_grp, 1)
        wd_mul(1)
        for k in range(4):
            nc.gpsimd.tensor_scalar(out=wd_grp[0][:, k], in0=w_view(wd_raw[0])[:, k], scalar1=1.0, scalar2=0.0, op0=MULT, op1=ADD)
        cast(1, 0)
        cast(1, 1)
        cast(2, 0)
        cast(2, 1)
        nc.scalar.copy(out=wd_grp[1][:], in_=w_view(wd_raw[1]))
        nc.vector.tensor_copy(out=scol[:], in_=sb[:])
        nc.vector.tensor_copy(out=tcol[:], in_=tb[:])
        nc.vector.tensor_scalar(out=bcol[:], in0=bb[:], scalar1=1.0 / 1.5, scalar2=None, op0=MULT)

        for slot in range(UNITS + 3):
            u_next, u_p, u_s, u_r, u_o = slot + 1, slot, slot - 1, slot - 2, slot - 3
            if slot + 3 < UNITS:
                cast(slot + 3, 0)
            if u_next < UNITS:
                xtr(u_next)
            if slot == 1:
                gbank = []
                for k in range(4):
                    bank = psum.tile([P, F], F32, name="gb%d" % k, tag=("rr0", "rr1", "oo0", "oo1")[k])
                    gbank.append(bank)
                    for g in range(2):
                        nc.tensor.matmul_mx(
                            out=bank[:],
                            lhsT=wd_codes[:, g, P * k:P * (k + 1)].bitcast(FP8X4),
                            lhsT_scale=wd_scales[:, g, P * k:P * (k + 1)],
                            rhs=w_codes[:, g, :].bitcast(FP8X4),
                            rhs_scale=w_scales[:, g, :],
                            start=(g == 0),
                            stop=(g == 1),
                        )
                for k in range(4):
                    nc.scalar.activation(out=gt_planes[:, k, :], in_=gbank[k][:], func=COPY, scale=tcol[:, k:k + 1])
            if 0 <= u_s < UNITS:
                ps(u_s)
                ilv(u_s)
            if 0 <= u_o < UNITS:
                otr(u_o)
                hrcopy(u_o)
            if slot == 2:
                nc.vector.tensor_copy(out=gt_grp[:], in_=gt_planes[:].rearrange("p k c -> p c k"))
                nc.vector.quantize_mx(out=gt_codes[:].bitcast(FP8X4), scales=gt_scales[:], in_=gt_grp[:].rearrange("p c k -> p (c k)"))
            if u_next < UNITS:
                xmul(u_next, 0)
                xmul(u_next, 1)
            if slot == 0:
                wquant(wd_codes, wd_scales, wd_grp, 0)
                wquant(wd_codes, wd_scales, wd_grp, 1)
            if 0 <= u_r < UNITS:
                rmm(u_r)
                zz(u_r)
            if u_p < UNITS:
                pmm(u_p)
                pout(u_p)
            if slot + 3 < UNITS:
                cast(slot + 3, 1)
            if 0 <= u_o < UNITS:
                maxmin(u_o)
            if u_next < UNITS:
                xq(u_next)
            if 0 <= u_s < UNITS:
                psquant(u_s)
